import numpy as np
import ml_dtypes


def mxq(x, axis, fmt="e4m3"):
    dtype, down = {"e4m3": (ml_dtypes.float8_e4m3fn, 7), "e5m2": (ml_dtypes.float8_e5m2, 14)}[fmt]
    v = np.moveaxis(np.asarray(x, np.float32).astype(ml_dtypes.bfloat16).astype(np.float64), axis, -1)
    blocks = v.reshape(v.shape[:-1] + (-1, 32))
    amax = np.abs(blocks).max(-1, keepdims=True)
    byte = np.maximum(np.where(amax > 0, np.frexp(amax)[1] - 1 + 127, 0) - down, 1)
    scale = np.exp2(byte - 127.0)
    codes = (blocks / scale).astype(np.float32).astype(dtype).astype(np.float64)
    return np.moveaxis((codes * scale).reshape(v.shape), -1, axis)


WIDE = False


def mx_kscale(k):
    if not WIDE:
        return np.ones(k)
    levels = np.array([10, -10, 5, -5, 0])
    if k % 512:
        return np.exp2(np.random.permutation(np.resize(levels, k // 32))).repeat(32)
    a = np.empty((k // 512, 16))
    for p in range(k // 512):
        a[p, :8] = np.random.permutation(np.resize(levels, 8))
        for g in range(8):
            far = levels[np.abs(levels - a[p, g]) >= 10]
            a[p, g + 8] = far[np.random.randint(len(far))]
    return np.exp2(a.ravel()).repeat(32)


def f64(x):
    return np.asarray(x).astype(np.float64)


def striped(idx):
    return np.tile(idx.reshape(-1, 16).T, (8, 1)).astype(np.uint16)


def unstriped(offs):
    return offs[:16].T.reshape(-1).astype(np.int64)


E2M1 = np.array([0.0, 0.5, 1.0, 1.5, 2.0, 3.0, 4.0, 6.0, -0.0, -0.5, -1.0, -1.5, -2.0, -3.0, -4.0, -6.0])


def pack_weight(w, fmt):
    k, n = w.shape
    w = f64(np.asarray(w, np.float32).astype(ml_dtypes.bfloat16)).reshape(k // 32, 32, n)
    amax = np.abs(w).max(1)
    if fmt == "e4m3":
        byte = np.frexp(amax)[1] - 1 + 127 - 7
    else:
        mant, ex = np.frexp(amax / 6.0)
        byte = np.where(mant > 0.5, ex, ex - 1) + 127
    byte = np.clip(np.where(amax > 0, byte, 1), 1, 254)
    scaled = (w * np.exp2(127.0 - byte)[:, None, :]).reshape(k, n).astype(np.float32)
    by_word = np.ascontiguousarray(scaled.reshape(k // 512, 128, 4, n).transpose(0, 1, 3, 2))
    if fmt == "e4m3":
        words = by_word.astype(ml_dtypes.float8_e4m3fn).view(np.uint8)
    else:
        c = by_word.astype(ml_dtypes.float4_e2m1fn).view(np.uint8) & 0xF
        words = (c[..., 0::2] | (c[..., 1::2] << 4)).reshape(k // 512, 128, 2 * n)
    return np.ascontiguousarray(words), np.ascontiguousarray(byte.astype(np.uint8).reshape(k // 512, 16, n))


def unpack_weight(words, scales, fmt):
    g, _, n = scales.shape
    words = np.ascontiguousarray(words).reshape(g, 128, n, -1)
    if fmt == "e4m3":
        vals = words.view(ml_dtypes.float8_e4m3fn).astype(np.float64)
    else:
        nib = np.empty((g, 128, n, 4), np.uint8)
        nib[..., 0::2] = words & 0xF
        nib[..., 1::2] = words >> 4
        vals = E2M1[nib]
    vals = vals * np.repeat(np.exp2(scales.astype(np.float64) - 127.0), 8, axis=1)[..., None]
    return vals.transpose(0, 1, 3, 2).reshape(g * 512, n)


def gelu(v):
    return 0.5 * v * (1.0 + np.tanh(np.sqrt(2.0 / np.pi) * (v + 0.044715 * v**3)))


K, T, S, H, P, N = 512, 4096, 1024, 1024, 512, 512

def setup_inputs():
    n = np.random.standard_normal
    s = mx_kscale(K)[:, None]
    u = mx_kscale(H)[:, None]
    tab_words, tab_scales = pack_weight(n((K, T)) * s, "e4m3")
    w3_words, w3_scales = pack_weight(n((K, H)) / np.sqrt(K) / s, "e2m1")
    wb_words, wb_scales = pack_weight(1.3 * n((H, N)) / np.sqrt(H) / u, "e4m3")
    return {
        "tab_words": tab_words, "tab_scales": tab_scales,
        "offs": striped(np.random.permutation(T)[:S]),
        "pos1": striped(np.random.permutation(S)[:P]),
        "pos2": striped(np.random.permutation(S)[:P]),
        "w1": (n((K, H)) / np.sqrt(K) / s).astype(np.float32),
        "w2": (n((K, H)) / np.sqrt(K) / s).astype(np.float32),
        "w3_words": w3_words, "w3_scales": w3_scales,
        "ga": (np.exp(0.3 * n(H)) * u[:, 0]).astype(np.float32),
        "gb": (np.exp(0.3 * n(H)) * u[:, 0]).astype(np.float32),
        "food": (n((H, P)) * u).astype(np.float32),
        "wa": (n((H, N)) / np.sqrt(H) / u).astype(np.float32),
        "wb_words": wb_words, "wb_scales": wb_scales,
    }

def reference(tab_words, tab_scales, offs, pos1, pos2, w1, w2, w3_words, w3_scales, ga, gb, food, wa, wb_words, wb_scales):
    v = unpack_weight(tab_words, tab_scales, "e4m3")[:, unstriped(offs)]
    w1q = mxq(f64(w1), 0, "e4m3")
    w2q = mxq(f64(w2), 0, "e4m3")
    w3 = unpack_weight(w3_words, w3_scales, "e2m1")
    h = np.maximum(w1q.T @ v + w3.T @ v, w2q.T @ v + w3.T @ v)
    xa = f64(ga)[:, None] * h[:, unstriped(pos1)] + f64(food)
    xb = f64(gb)[:, None] * np.tanh(h[:, unstriped(pos2)])
    wb = unpack_weight(wb_words, wb_scales, "e4m3")
    ya = mxq(f64(wa), 0, "e4m3").T @ mxq(xa, 0, "e4m3")
    yb = wb.T @ mxq(xb, 0, "e4m3")
    return ya * yb + yb

@@ -1,0 +1,257 @@
+from contextlib import ExitStack
+
+import concourse.mybir as mybir
+
+K, T, S, H, J, N = 512, 4096, 1024, 1024, 512, 512
+FLOPS = 2 * (4 * K * H * S + 2 * H * N * J)
+
+F32 = mybir.dt.float32
+BF16 = mybir.dt.bfloat16
+I32 = mybir.dt.int32
+U32 = mybir.dt.uint32
+U16 = mybir.dt.uint16
+U8 = mybir.dt.uint8
+FP8X4 = mybir.dt.float8_e4m3fn_x4
+FP4X4 = mybir.dt.float4_e2m1fn_x4
+ALU = mybir.AluOpType
+ACT = mybir.ActivationFunctionType
+
+P = 128
+PACK = 4
+BANK = 512
+PASSES = H // (P * PACK)
+ROW_TILES = H // P
+HALVES = S // BANK
+N_TILES = N // P
+
+
+def tile_list_allergen_component_reading_kernel(
+    tc, tab_words, tab_scales, offs, pos1, pos2, w1, w2, w3_words, w3_scales,
+    ga, gb, food, wa, wb_words, wb_scales, out,
+):
+    nc = tc.nc
+    with ExitStack() as ctx:
+        keep = ctx.enter_context(tc.tile_pool(name="keep", bufs=1))
+        staged = ctx.enter_context(tc.tile_pool(name="staged", bufs=4))
+        work = ctx.enter_context(tc.tile_pool(name="work", bufs=3))
+        psum = ctx.enter_context(tc.psum_pool(name="psum", bufs=1))
+
+        def kept(name, shape, dtype):
+            return keep.tile(shape, dtype, name=name, align_bytes=64)
+
+        def stage(name, shape, dtype):
+            return staged.tile(shape, dtype, name=name, tag="staged", align_bytes=64)
+
+        def load_scale_rows(queue, plane, rows):
+            nc.vector.memset(plane[:].bitcast(I32), 0)
+            for q in range(4):
+                queue.dma_start(plane[32 * q : 32 * q + 4].bitcast(I32), rows[4 * q : 4 * q + 4].bitcast(I32))
+
+        def load_rows(name, matrix, b):
+            raw = stage(name, [P, PACK, BANK], F32)
+            nc.sync.dma_start(raw[:], matrix[BANK * b : BANK * (b + 1), :].rearrange("(p i) c -> p i c", i=PACK))
+            return raw
+
+        def load_weight_columns(name, w, b):
+            raw = stage(name, [P, PACK, BANK], F32)
+            nc.sync.dma_start(raw[:], w[:, BANK * b : BANK * (b + 1)].rearrange("(p i) c -> p i c", i=PACK))
+            return raw
+
+        def quantise(name, grouped, width):
+            codes = kept(name + "_codes", [P, width], U32)
+            scales = kept(name + "_scales", [P, width], U8)
+            nc.vector.quantize_mx(out=codes[:].bitcast(FP8X4), scales=scales[:], in_=grouped)
+            return codes, scales
+
+        offs_t = kept("offs_t", [P, S // 16], U16)
+        nc.sync.dma_start(offs_t[:], offs)
+        pos1_t = kept("pos1_t", [P, J // 16], U16)
+        nc.sync.dma_start(pos1_t[:], pos1)
+        pos2_t = kept("pos2_t", [P, J // 16], U16)
+        nc.sync.dma_start(pos2_t[:], pos2)
+        ga_t = keep.tile([P, PASSES, PACK], F32, name="ga_t", tag="gain")
+        nc.sync.dma_start(ga_t[:], ga.rearrange("(b p i) -> p b i", p=P, i=PACK))
+        w3_raw = stage("w3_raw", [P, 2 * H], U8)
+        nc.sync.dma_start(w3_raw[:].bitcast(I32), w3_words[0].bitcast(I32))
+        tab_w = kept("tab_w", [P, T], U32)
+        nc.sync.dma_start(tab_w[:].bitcast(I32), tab_words[0].rearrange("p t i -> p (t i)").bitcast(I32))
+        w3s_raw = stage("w3s_raw", [P, H], U8)
+        load_scale_rows(nc.gpsimd, w3s_raw, w3_scales[0])
+        tab_s = kept("tab_s", [P, T], U8)
+        load_scale_rows(nc.scalar, tab_s, tab_scales[0])
+        w_raw = {}
+        w_raw[1, 0] = load_weight_columns("w1_raw0", w1, 0)
+        w_raw[2, 0] = load_weight_columns("w2_raw0", w2, 0)
+
+        ga_wide = kept("ga_wide", [P, ROW_TILES, J], F32)
+        for b in range(PASSES):
+            nc.scalar.copy(ga_wide[:, PACK * b : PACK * (b + 1), :], ga_t[:, b, :].unsqueeze(2).to_broadcast([P, PACK, J]))
+
+        gb_t = keep.tile([P, PASSES, PACK], F32, name="gb_t", tag="gain")
+        nc.sync.dma_start(gb_t[:], gb.rearrange("(b p i) -> p b i", p=P, i=PACK))
+
+        w3_codes = kept("w3_codes", [P, 2 * H], U8)
+        nc.vector.tensor_copy(
+            w3_codes[:].rearrange("p (b t m y) -> p b t m y", b=PASSES, t=PACK, y=2),
+            w3_raw[:].rearrange("p (b m t y) -> p b t m y", b=PASSES, t=PACK, y=2),
+        )
+
+        w3_sc = kept("w3_sc", [P, H], U8)
+        nc.vector.tensor_copy(
+            w3_sc[:].rearrange("p (b t m) -> p b t m", b=PASSES, t=PACK),
+            w3s_raw[:].rearrange("p (b m t) -> p b t m", b=PASSES, t=PACK),
+        )
+
+        w_raw[1, 1] = load_weight_columns("w1_raw1", w1, 1)
+        w_raw[2, 1] = load_weight_columns("w2_raw1", w2, 1)
+
+        v_codes, v_scales = [], []
+        for half in range(HALVES):
+            cols = offs_t[:, half * (BANK // 16) : (half + 1) * (BANK // 16)]
+            codes = kept(f"v_codes{half}", [P, BANK], U32)
+            nc.vector.tensor_copy(codes[:], tab_w[:].indirect(cols))
+            scales = kept(f"v_scales{half}", [P, BANK], U8)
+            nc.vector.tensor_copy(scales[:], tab_s[:].indirect(cols))
+            v_codes.append(codes)
+            v_scales.append(scales)
+
+        wq = {}
+
+        def prepare_weight(which, b, u, on_vector):
+            grouped = work.tile([P, 2, P, PACK], BF16, name="w_grouped", tag="w_grouped", align_bytes=64)
+            src = w_raw[which, b][:].rearrange("p i (m t) -> p m i t", t=PACK)[:, :, :, 2 * u : 2 * u + 2]
+            dst = grouped[:].rearrange("p t m i -> p m i t")
+            if on_vector:
+                nc.vector.tensor_copy(dst, src)
+            else:
+                nc.scalar.copy(dst, src)
+            wq[which, b, u] = quantise(f"w{which}_{b}{u}", grouped[:].rearrange("p t m i -> p (t m i)"), 2 * P)
+
+        def woven(tile):
+            return tile[:].rearrange("p (c e) t -> p c t e", e=2)
+
+        def planes(tile):
+            return tile[:].rearrange("p t (c e) -> p c t e", e=2)
+
+        def flat(tile):
+            return tile[:].rearrange("p c t -> p (c t)")
+
+        def bank(index):
+            return psum.tile([P, BANK], F32, name=f"bank{index}", tag=f"bank{index}")
+
+        def arm(which, r, half):
+            b, t = divmod(r, PACK)
+            codes, scales = wq[which, b, t // 2]
+            cols = slice(P * (t % 2), P * (t % 2 + 1))
+            acc = bank(4 * (which - 1) + 2 * (r % 2) + half)
+            nc.tensor.matmul_mx(
+                out=acc[:], lhsT=codes[:, cols].bitcast(FP8X4), lhsT_scale=scales[:, cols],
+                rhs=v_codes[half][:].bitcast(FP8X4), rhs_scale=v_scales[half][:], start=True, stop=False,
+            )
+            nc.tensor.matmul_mx(
+                out=acc[:], lhsT=w3_codes[:, 2 * P * r : 2 * P * (r + 1)].bitcast(FP4X4),
+                lhsT_scale=w3_sc[:, P * r : P * (r + 1)],
+                rhs=v_codes[half][:].bitcast(FP8X4), rhs_scale=v_scales[half][:], start=False, stop=True,
+            )
+            return acc
+
+        first_arm, h_tiles = {}, {}
+
+        def first_arm_out(r):
+            first_arm[r] = work.tile([P, S], F32, name="first_arm", tag="first_arm")
+            for half in range(HALVES):
+                acc = arm(1, r, half)
+                nc.scalar.copy(first_arm[r][:, BANK * half : BANK * (half + 1)], acc[:])
+
+        def larger_arm(r):
+            h_tiles[r] = work.tile([P, S], F32, name="h", tag="h")
+            for half in range(HALVES):
+                cols = slice(BANK * half, BANK * (half + 1))
+                acc = arm(2, r, half)
+                nc.vector.tensor_tensor(h_tiles[r][:, cols], acc[:], first_arm[r][:, cols], ALU.max)
+
+        gained_a = [kept(f"gained_a{b}", [P, PACK, J], F32) for b in range(PASSES)]
+        xb_planes = [kept(f"xb_planes{b}", [P, PACK, J], BF16) for b in range(PASSES)]
+
+        def pick(r):
+            b, t = divmod(r, PACK)
+            picked = work.tile([P, J], F32, name="picked", tag="picked")
+            nc.vector.tensor_copy(picked[:], h_tiles[r][:].indirect(pos2_t[:]))
+            nc.vector.tensor_tensor(gained_a[b][:, t, :], h_tiles[r][:].indirect(pos1_t[:]), ga_wide[:, r, :], ALU.mult)
+            bent = work.tile([P, J], F32, name="bent", tag="bent")
+            nc.scalar.activation(bent[:], picked[:], ACT.Tanh)
+            nc.scalar.activation(xb_planes[b][:, t, :], bent[:], ACT.Copy, scale=gb_t[:, b, t : t + 1])
+
+        xq, food_raw, wa_raw, waq = {}, {}, {}, {}
+
+        def finish_x(b):
+            xb = kept(f"xb{b}", [P, J, PACK], BF16)
+            nc.scalar.copy(woven(xb), planes(xb_planes[b]))
+            xa = kept(f"xa{b}", [P, J, PACK], BF16)
+            nc.vector.tensor_tensor(woven(xa), planes(gained_a[b]), planes(food_raw[b]), ALU.add)
+            xq["a", b] = quantise(f"xa{b}", flat(xa), J)
+            xq["b", b] = quantise(f"xb{b}", flat(xb), J)
+
+        def prepare_wa(b):
+            grouped = kept(f"wa_grouped{b}", [P, N, PACK], BF16)
+            for part in range(2):
+                c = slice(P * part, P * (part + 1))
+                nc.scalar.copy(woven(grouped)[:, c], planes(wa_raw[b])[:, c])
+            waq[b] = quantise(f"wa{b}", flat(grouped), N)
+
+        prepare_weight(1, 0, 0, False)
+        prepare_weight(1, 0, 1, False)
+        first_arm_out(0)
+        prepare_weight(2, 0, 0, True)
+        prepare_weight(2, 0, 1, False)
+        food_raw[0] = load_rows("food0", food, 0)
+        larger_arm(0)
+        for r in range(ROW_TILES):
+            if r + 1 < ROW_TILES:
+                first_arm_out(r + 1)
+                larger_arm(r + 1)
+            pick(r)
+            if r < 2:
+                prepare_weight(1, 1, r, False)
+                prepare_weight(2, 1, r, False)
+            if r == 1:
+                wa_raw[0] = load_rows("wa0", wa, 0)
+                wa_raw[1] = load_rows("wa1", wa, 1)
+            if r == 3:
+                finish_x(0)
+            if r in (4, 5):
+                prepare_wa(r - 4)
+            if r == 5:
+                food_raw[1] = load_rows("food1", food, 1)
+                wb_codes = stage("wb_codes", [P, PASSES, N], U32)
+                nc.sync.dma_start(wb_codes[:].bitcast(I32), wb_words.rearrange("a p c i -> p a (c i)").bitcast(I32))
+                wb_sc = stage("wb_sc", [P, PASSES, N], U8)
+                load_scale_rows(nc.sync, wb_sc, wb_scales.rearrange("a q c -> q a c"))
+
+        def second_stage(b, ya, yb):
+            for n in range(N_TILES):
+                cols = slice(P * n, P * (n + 1))
+                nc.tensor.matmul_mx(
+                    out=ya[n][:], lhsT=waq[b][0][:, cols].bitcast(FP8X4), lhsT_scale=waq[b][1][:, cols],
+                    rhs=xq["a", b][0][:].bitcast(FP8X4), rhs_scale=xq["a", b][1][:],
+                    start=(b == 0), stop=(b == PASSES - 1),
+                )
+            for n in range(N_TILES):
+                cols = slice(P * n, P * (n + 1))
+                nc.tensor.matmul_mx(
+                    out=yb[n][:], lhsT=wb_codes[:, b, cols].bitcast(FP8X4), lhsT_scale=wb_sc[:, b, cols],
+                    rhs=xq["b", b][0][:].bitcast(FP8X4), rhs_scale=xq["b", b][1][:],
+                    start=(b == 0), stop=(b == PASSES - 1),
+                )
+
+        ya = [bank(n) for n in range(N_TILES)]
+        yb = [bank(N_TILES + n) for n in range(N_TILES)]
+        second_stage(0, ya, yb)
+        finish_x(1)
+        second_stage(1, ya, yb)
+        for n in range(N_TILES):
+            ya_plus = kept(f"ya_plus{n}", [P, J], F32)
+            nc.scalar.activation(ya_plus[:], ya[n][:], ACT.Copy, bias=1.0)
+            result = kept(f"result{n}", [P, J], F32)
+            nc.vector.tensor_tensor(result[:], yb[n][:], ya_plus[:], ALU.mult)
+            nc.sync.dma_start(out[P * n : P * (n + 1), :], result[:])

@@ -63,29 +63,29 @@ def tile_list_allergen_component_reading_kernel(
             nc.vector.quantize_mx(out=codes[:].bitcast(FP8X4), scales=scales[:], in_=grouped)
             return codes, scales
 
-        offs_t = kept("offs_t", [P, S // 16], U16)
-        nc.sync.dma_start(offs_t[:], offs)
-        pos1_t = kept("pos1_t", [P, J // 16], U16)
-        nc.sync.dma_start(pos1_t[:], pos1)
-        pos2_t = kept("pos2_t", [P, J // 16], U16)
-        nc.sync.dma_start(pos2_t[:], pos2)
-        ga_t = keep.tile([P, PASSES, PACK], F32, name="ga_t", tag="gain")
-        nc.sync.dma_start(ga_t[:], ga.rearrange("(b p i) -> p b i", p=P, i=PACK))
         w3_raw = stage("w3_raw", [P, 2 * H], U8)
         nc.sync.dma_start(w3_raw[:].bitcast(I32), w3_words[0].bitcast(I32))
+        offs_t = kept("offs_t", [P, S // 16], U16)
+        nc.sync.dma_start(offs_t[:], offs)
+        ga_t = keep.tile([P, PASSES, PACK], F32, name="ga_t", tag="gain")
+        nc.sync.dma_start(ga_t[:], ga.rearrange("(b p i) -> p b i", p=P, i=PACK))
+        pos2_t = kept("pos2_t", [P, J // 16], U16)
+        nc.sync.dma_start(pos2_t[:], pos2)
+        pos1_t = kept("pos1_t", [P, J // 16], U16)
+        nc.sync.dma_start(pos1_t[:], pos1)
         tab_w = kept("tab_w", [P, T], U32)
         nc.sync.dma_start(tab_w[:].bitcast(I32), tab_words[0].rearrange("p t i -> p (t i)").bitcast(I32))
-        w3s_raw = stage("w3s_raw", [P, H], U8)
-        load_scale_rows(nc.gpsimd, w3s_raw, w3_scales[0])
         tab_s = kept("tab_s", [P, T], U8)
         load_scale_rows(nc.scalar, tab_s, tab_scales[0])
+        w3s_raw = keep.tile([P, H], U8, name="w3s_raw", tag="scale_rows", align_bytes=64)
+        load_scale_rows(nc.scalar, w3s_raw, w3_scales[0])
         w_raw = {}
         w_raw[1, 0] = load_weight_columns("w1_raw0", w1, 0)
         w_raw[2, 0] = load_weight_columns("w2_raw0", w2, 0)
 
         ga_wide = kept("ga_wide", [P, ROW_TILES, J], F32)
         for b in range(PASSES):
-            nc.scalar.copy(ga_wide[:, PACK * b : PACK * (b + 1), :], ga_t[:, b, :].unsqueeze(2).to_broadcast([P, PACK, J]))
+            nc.vector.tensor_copy(ga_wide[:, PACK * b : PACK * (b + 1), :], ga_t[:, b, :].unsqueeze(2).to_broadcast([P, PACK, J]))
 
         gb_t = keep.tile([P, PASSES, PACK], F32, name="gb_t", tag="gain")
         nc.sync.dma_start(gb_t[:], gb.rearrange("(b p i) -> p b i", p=P, i=PACK))
@@ -136,14 +136,22 @@ def tile_list_allergen_component_reading_kernel(
         def flat(tile):
             return tile[:].rearrange("p c t -> p (c t)")
 
-        def bank(index):
-            return psum.tile([P, BANK], F32, name=f"bank{index}", tag=f"bank{index}")
+        banks = [psum.tile([P, BANK], F32, name=f"bank{index}") for index in range(8)]
+
+        def arm_bank(which, r, half):
+            if r == 0:
+                pair = which - 1
+            elif which == 1:
+                pair = 1
+            else:
+                pair = 2 + r % 2
+            return banks[2 * pair + half]
 
         def arm(which, r, half):
             b, t = divmod(r, PACK)
             codes, scales = wq[which, b, t // 2]
             cols = slice(P * (t % 2), P * (t % 2 + 1))
-            acc = bank(4 * (which - 1) + 2 * (r % 2) + half)
+            acc = arm_bank(which, r, half)
             nc.tensor.matmul_mx(
                 out=acc[:], lhsT=codes[:, cols].bitcast(FP8X4), lhsT_scale=scales[:, cols],
                 rhs=v_codes[half][:].bitcast(FP8X4), rhs_scale=v_scales[half][:], start=True, stop=False,
@@ -158,7 +166,7 @@ def tile_list_allergen_component_reading_kernel(
         first_arm, h_tiles = {}, {}
 
         def first_arm_out(r):
-            first_arm[r] = work.tile([P, S], F32, name="first_arm", tag="first_arm")
+            first_arm[r] = work.tile([P, S], F32, name="first_arm", tag="first_arm", align_bytes=64)
             for half in range(HALVES):
                 acc = arm(1, r, half)
                 nc.scalar.copy(first_arm[r][:, BANK * half : BANK * (half + 1)], acc[:])
@@ -173,24 +181,29 @@ def tile_list_allergen_component_reading_kernel(
         gained_a = [kept(f"gained_a{b}", [P, PACK, J], F32) for b in range(PASSES)]
         xb_planes = [kept(f"xb_planes{b}", [P, PACK, J], BF16) for b in range(PASSES)]
 
-        def pick(r):
+        def pick_b(r):
             b, t = divmod(r, PACK)
             picked = work.tile([P, J], F32, name="picked", tag="picked")
             nc.vector.tensor_copy(picked[:], h_tiles[r][:].indirect(pos2_t[:]))
-            nc.vector.tensor_tensor(gained_a[b][:, t, :], h_tiles[r][:].indirect(pos1_t[:]), ga_wide[:, r, :], ALU.mult)
             bent = work.tile([P, J], F32, name="bent", tag="bent")
             nc.scalar.activation(bent[:], picked[:], ACT.Tanh)
             nc.scalar.activation(xb_planes[b][:, t, :], bent[:], ACT.Copy, scale=gb_t[:, b, t : t + 1])
 
+        def pick_a(r):
+            b, t = divmod(r, PACK)
+            nc.vector.tensor_tensor(gained_a[b][:, t, :], h_tiles[r][:].indirect(pos1_t[:]), ga_wide[:, r, :], ALU.mult)
+
         xq, food_raw, wa_raw, waq = {}, {}, {}, {}
 
-        def finish_x(b):
+        def weave_xb(b):
             xb = kept(f"xb{b}", [P, J, PACK], BF16)
-            nc.scalar.copy(woven(xb), planes(xb_planes[b]))
-            xa = kept(f"xa{b}", [P, J, PACK], BF16)
+            for part in range(2):
+                c = slice(P * part, P * (part + 1))
+                nc.scalar.copy(woven(xb)[:, c], planes(xb_planes[b])[:, c])
+            return xb
+
+        def weave_xa(b, xa):
             nc.vector.tensor_tensor(woven(xa), planes(gained_a[b]), planes(food_raw[b]), ALU.add)
-            xq["a", b] = quantise(f"xa{b}", flat(xa), J)
-            xq["b", b] = quantise(f"xb{b}", flat(xb), J)
 
         def prepare_wa(b):
             grouped = kept(f"wa_grouped{b}", [P, N, PACK], BF16)
@@ -200,58 +213,61 @@ def tile_list_allergen_component_reading_kernel(
             waq[b] = quantise(f"wa{b}", flat(grouped), N)
 
         prepare_weight(1, 0, 0, False)
-        prepare_weight(1, 0, 1, False)
         first_arm_out(0)
         prepare_weight(2, 0, 0, True)
-        prepare_weight(2, 0, 1, False)
-        food_raw[0] = load_rows("food0", food, 0)
         larger_arm(0)
-        for r in range(ROW_TILES):
-            if r + 1 < ROW_TILES:
-                first_arm_out(r + 1)
-                larger_arm(r + 1)
-            pick(r)
-            if r < 2:
-                prepare_weight(1, 1, r, False)
-                prepare_weight(2, 1, r, False)
-            if r == 1:
-                wa_raw[0] = load_rows("wa0", wa, 0)
-                wa_raw[1] = load_rows("wa1", wa, 1)
-            if r == 3:
-                finish_x(0)
-            if r in (4, 5):
-                prepare_wa(r - 4)
-            if r == 5:
-                food_raw[1] = load_rows("food1", food, 1)
-                wb_codes = stage("wb_codes", [P, PASSES, N], U32)
-                nc.sync.dma_start(wb_codes[:].bitcast(I32), wb_words.rearrange("a p c i -> p a (c i)").bitcast(I32))
-                wb_sc = stage("wb_sc", [P, PASSES, N], U8)
-                load_scale_rows(nc.sync, wb_sc, wb_scales.rearrange("a q c -> q a c"))
+        prepare_weight(1, 0, 1, False)
+        prepare_weight(2, 0, 1, False)
+        wa_raw[0] = load_rows("wa0", wa, 0)
+        wa_raw[1] = load_rows("wa1", wa, 1)
+        food_raw[0] = load_rows("food0", food, 0)
+        food_raw[1] = load_rows("food1", food, 1)
+        wb_codes = stage("wb_codes", [P, PASSES, N], U32)
+        nc.sync.dma_start(wb_codes[:].bitcast(I32), wb_words.rearrange("a p c i -> p a (c i)").bitcast(I32))
+        wb_sc = keep.tile([P, PASSES, N], U8, name="wb_sc", tag="scale_rows", align_bytes=64)
+        load_scale_rows(nc.sync, wb_sc, wb_scales.rearrange("a q c -> q a c"))
+        for r in range(ROW_TILES - 1):
+            first_arm_out(r + 1)
+            larger_arm(r + 1)
+            pick_b(r)
+            pick_a(r)
+            if r in (0, 2):
+                prepare_weight(1, 1, r // 2, False)
+            if r in (1, 3):
+                prepare_weight(2, 1, r // 2, False)
+            if r == 4:
+                xq["b", 0] = quantise("xb0", flat(weave_xb(0)), J)
+            if r in (5, 6):
+                prepare_wa(r - 5)
 
-        def second_stage(b, ya, yb):
+        def product(acc, lhs_codes, lhs_scales, x, b):
             for n in range(N_TILES):
                 cols = slice(P * n, P * (n + 1))
                 nc.tensor.matmul_mx(
-                    out=ya[n][:], lhsT=waq[b][0][:, cols].bitcast(FP8X4), lhsT_scale=waq[b][1][:, cols],
-                    rhs=xq["a", b][0][:].bitcast(FP8X4), rhs_scale=xq["a", b][1][:],
-                    start=(b == 0), stop=(b == PASSES - 1),
-                )
-            for n in range(N_TILES):
-                cols = slice(P * n, P * (n + 1))
-                nc.tensor.matmul_mx(
-                    out=yb[n][:], lhsT=wb_codes[:, b, cols].bitcast(FP8X4), lhsT_scale=wb_sc[:, b, cols],
-                    rhs=xq["b", b][0][:].bitcast(FP8X4), rhs_scale=xq["b", b][1][:],
+                    out=acc[n][:], lhsT=lhs_codes[:, cols].bitcast(FP8X4), lhsT_scale=lhs_scales[:, cols],
+                    rhs=x[0][:].bitcast(FP8X4), rhs_scale=x[1][:],
                     start=(b == 0), stop=(b == PASSES - 1),
                 )
 
-        ya = [bank(n) for n in range(N_TILES)]
-        yb = [bank(N_TILES + n) for n in range(N_TILES)]
-        second_stage(0, ya, yb)
-        finish_x(1)
-        second_stage(1, ya, yb)
+        yb = [banks[n] for n in (0, 1, 4, 5)]
+        ya = [banks[n] for n in (2, 3, 6, 7)]
+        last = ROW_TILES - 1
+        product(yb, wb_codes[:, 0, :], wb_sc[:, 0, :], xq["b", 0], 0)
+        pick_b(last)
+        xa0 = first_arm[last][:].bitcast(BF16).rearrange("p (c t) -> p c t", t=PACK)
+        weave_xa(0, xa0)
+        pick_a(last)
+        xq["a", 0] = quantise("xa0", flat(xa0), J)
+        product(ya, waq[0][0], waq[0][1], xq["a", 0], 0)
+        xa1 = kept("xa1", [P, J, PACK], BF16)
+        weave_xa(1, xa1)
+        xq["b", 1] = quantise("xb1", flat(weave_xb(1)), J)
+        product(yb, wb_codes[:, 1, :], wb_sc[:, 1, :], xq["b", 1], 1)
+        xq["a", 1] = quantise("xa1", flat(xa1), J)
+        product(ya, waq[1][0], waq[1][1], xq["a", 1], 1)
         for n in range(N_TILES):
-            ya_plus = kept(f"ya_plus{n}", [P, J], F32)
-            nc.scalar.activation(ya_plus[:], ya[n][:], ACT.Copy, bias=1.0)
+            yb_out = kept(f"yb_out{n}", [P, J], F32)
+            nc.scalar.copy(yb_out[:], yb[n][:])
             result = kept(f"result{n}", [P, J], F32)
-            nc.vector.tensor_tensor(result[:], yb[n][:], ya_plus[:], ALU.mult)
+            nc.vector.scalar_tensor_tensor(result[:], ya[n][:], 1.0, yb_out[:], ALU.add, ALU.mult)
             nc.sync.dma_start(out[P * n : P * (n + 1), :], result[:])

@@ -63,32 +63,34 @@ def tile_list_allergen_component_reading_kernel(
             nc.vector.quantize_mx(out=codes[:].bitcast(FP8X4), scales=scales[:], in_=grouped)
             return codes, scales
 
-        w3_raw = stage("w3_raw", [P, 2 * H], U8)
-        nc.sync.dma_start(w3_raw[:].bitcast(I32), w3_words[0].bitcast(I32))
         offs_t = kept("offs_t", [P, S // 16], U16)
         nc.sync.dma_start(offs_t[:], offs)
-        ga_t = keep.tile([P, PASSES, PACK], F32, name="ga_t", tag="gain")
-        nc.sync.dma_start(ga_t[:], ga.rearrange("(b p i) -> p b i", p=P, i=PACK))
+        w3_raw = stage("w3_raw", [P, 2 * H], U8)
+        nc.sync.dma_start(w3_raw[:].bitcast(I32), w3_words[0].bitcast(I32))
+        tab_w = kept("tab_w", [P, T], U32)
+        tab_dram = tab_words[0].rearrange("p t i -> p (t i)").bitcast(I32)
+        nc.sync.dma_start(tab_w[:, : T // 2].bitcast(I32), tab_dram[:, : T // 2])
+        tab_s = kept("tab_s", [P, T], U8)
+        load_scale_rows(nc.sync, tab_s, tab_scales[0])
+        w_raw = {}
+        w_raw[1, 0] = load_weight_columns("w1_raw0", w1, 0)
+        w3s_raw = kept("w3s_raw", [P, H], U8)
+        load_scale_rows(nc.sync, w3s_raw, w3_scales[0])
+        nc.sync.dma_start(tab_w[:, T // 2 :].bitcast(I32), tab_dram[:, T // 2 :])
         pos2_t = kept("pos2_t", [P, J // 16], U16)
         nc.sync.dma_start(pos2_t[:], pos2)
         pos1_t = kept("pos1_t", [P, J // 16], U16)
         nc.sync.dma_start(pos1_t[:], pos1)
-        tab_w = kept("tab_w", [P, T], U32)
-        nc.sync.dma_start(tab_w[:].bitcast(I32), tab_words[0].rearrange("p t i -> p (t i)").bitcast(I32))
-        tab_s = kept("tab_s", [P, T], U8)
-        load_scale_rows(nc.scalar, tab_s, tab_scales[0])
-        w3s_raw = keep.tile([P, H], U8, name="w3s_raw", tag="scale_rows", align_bytes=64)
-        load_scale_rows(nc.scalar, w3s_raw, w3_scales[0])
-        w_raw = {}
-        w_raw[1, 0] = load_weight_columns("w1_raw0", w1, 0)
         w_raw[2, 0] = load_weight_columns("w2_raw0", w2, 0)
+        ga_t = kept("ga_t", [P, PASSES, PACK], F32)
+        nc.scalar.dma_start(ga_t[:], ga.rearrange("(b p i) -> p b i", p=P, i=PACK))
+        gb_t = kept("gb_t", [P, PASSES, PACK], F32)
+        nc.scalar.dma_start(gb_t[:], gb.rearrange("(b p i) -> p b i", p=P, i=PACK))
 
         ga_wide = kept("ga_wide", [P, ROW_TILES, J], F32)
-        for b in range(PASSES):
-            nc.vector.tensor_copy(ga_wide[:, PACK * b : PACK * (b + 1), :], ga_t[:, b, :].unsqueeze(2).to_broadcast([P, PACK, J]))
-
-        gb_t = keep.tile([P, PASSES, PACK], F32, name="gb_t", tag="gain")
-        nc.sync.dma_start(gb_t[:], gb.rearrange("(b p i) -> p b i", p=P, i=PACK))
+        ga_spread = [ga_t[:, b, :].unsqueeze(2).to_broadcast([P, PACK, J]) for b in range(PASSES)]
+        nc.scalar.activation(ga_wide[:, :PACK, :], ga_spread[0], ACT.Copy)
+        nc.scalar.activation(ga_wide[:, PACK:, :], ga_spread[1], ACT.Copy)
 
         w3_codes = kept("w3_codes", [P, 2 * H], U8)
         nc.vector.tensor_copy(
@@ -117,14 +119,15 @@ def tile_list_allergen_component_reading_kernel(
 
         wq = {}
 
-        def prepare_weight(which, b, u, on_vector):
-            grouped = work.tile([P, 2, P, PACK], BF16, name="w_grouped", tag="w_grouped", align_bytes=64)
+        def prepare_weight(which, b, u, on_vector, grouped=None):
+            if grouped is None:
+                grouped = work.tile([P, 2, P, PACK], BF16, name="w_grouped", tag="w_grouped", align_bytes=64)
             src = w_raw[which, b][:].rearrange("p i (m t) -> p m i t", t=PACK)[:, :, :, 2 * u : 2 * u + 2]
             dst = grouped[:].rearrange("p t m i -> p m i t")
             if on_vector:
                 nc.vector.tensor_copy(dst, src)
             else:
-                nc.scalar.copy(dst, src)
+                nc.scalar.activation(dst, src, ACT.Copy)
             wq[which, b, u] = quantise(f"w{which}_{b}{u}", grouped[:].rearrange("p t m i -> p (t m i)"), 2 * P)
 
         def woven(tile):
@@ -142,7 +145,7 @@ def tile_list_allergen_component_reading_kernel(
             if r == 0:
                 pair = which - 1
             elif which == 1:
-                pair = 1
+                pair = 1 if r < 3 else r % 2
             else:
                 pair = 2 + r % 2
             return banks[2 * pair + half]
@@ -166,7 +169,7 @@ def tile_list_allergen_component_reading_kernel(
         first_arm, h_tiles = {}, {}
 
         def first_arm_out(r):
-            first_arm[r] = work.tile([P, S], F32, name="first_arm", tag="first_arm", align_bytes=64)
+            first_arm[r] = work.tile([P, S], F32, name="first_arm", tag="first_arm", align_bytes=64, bufs=5)
             for half in range(HALVES):
                 acc = arm(1, r, half)
                 nc.scalar.copy(first_arm[r][:, BANK * half : BANK * (half + 1)], acc[:])
@@ -183,10 +186,10 @@ def tile_list_allergen_component_reading_kernel(
 
         def pick_b(r):
             b, t = divmod(r, PACK)
-            picked = work.tile([P, J], F32, name="picked", tag="picked")
-            nc.vector.tensor_copy(picked[:], h_tiles[r][:].indirect(pos2_t[:]))
+            picked = work.tile([P, J], F32, name="picked_b", tag="picked_b")[:]
+            nc.vector.tensor_copy(picked, h_tiles[r][:].indirect(pos2_t[:]))
             bent = work.tile([P, J], F32, name="bent", tag="bent")
-            nc.scalar.activation(bent[:], picked[:], ACT.Tanh)
+            nc.scalar.activation(bent[:], picked, ACT.Tanh)
             nc.scalar.activation(xb_planes[b][:, t, :], bent[:], ACT.Copy, scale=gb_t[:, b, t : t + 1])
 
         def pick_a(r):
@@ -205,40 +208,44 @@ def tile_list_allergen_component_reading_kernel(
         def weave_xa(b, xa):
             nc.vector.tensor_tensor(woven(xa), planes(gained_a[b]), planes(food_raw[b]), ALU.add)
 
-        def prepare_wa(b):
-            grouped = kept(f"wa_grouped{b}", [P, N, PACK], BF16)
+        def prepare_wa(b, grouped):
             for part in range(2):
                 c = slice(P * part, P * (part + 1))
                 nc.scalar.copy(woven(grouped)[:, c], planes(wa_raw[b])[:, c])
             waq[b] = quantise(f"wa{b}", flat(grouped), N)
+
+        def spent_half(r, half):
+            spent = first_arm[r][:, BANK * half : BANK * (half + 1)]
+            return spent.bitcast(BF16).rearrange("p (t m i) -> p t m i", t=2, i=PACK)
+
+        def spent_whole(r):
+            return first_arm[r][:].bitcast(BF16).rearrange("p (c t) -> p c t", t=PACK)
 
         prepare_weight(1, 0, 0, False)
         first_arm_out(0)
         prepare_weight(2, 0, 0, True)
         larger_arm(0)
         prepare_weight(1, 0, 1, False)
-        prepare_weight(2, 0, 1, False)
+        prepare_weight(2, 0, 1, False, spent_half(0, 0))
         wa_raw[0] = load_rows("wa0", wa, 0)
         wa_raw[1] = load_rows("wa1", wa, 1)
         food_raw[0] = load_rows("food0", food, 0)
         food_raw[1] = load_rows("food1", food, 1)
         wb_codes = stage("wb_codes", [P, PASSES, N], U32)
         nc.sync.dma_start(wb_codes[:].bitcast(I32), wb_words.rearrange("a p c i -> p a (c i)").bitcast(I32))
-        wb_sc = keep.tile([P, PASSES, N], U8, name="wb_sc", tag="scale_rows", align_bytes=64)
+        wb_sc = kept("wb_sc", [P, PASSES, N], U8)
         load_scale_rows(nc.sync, wb_sc, wb_scales.rearrange("a q c -> q a c"))
         for r in range(ROW_TILES - 1):
             first_arm_out(r + 1)
             larger_arm(r + 1)
             pick_b(r)
             pick_a(r)
-            if r in (0, 2):
-                prepare_weight(1, 1, r // 2, False)
-            if r in (1, 3):
-                prepare_weight(2, 1, r // 2, False)
+            if r < 4:
+                prepare_weight(1 + r % 2, 1, r // 2, False, spent_half(r, 1))
             if r == 4:
                 xq["b", 0] = quantise("xb0", flat(weave_xb(0)), J)
             if r in (5, 6):
-                prepare_wa(r - 5)
+                prepare_wa(r - 5, spent_whole(r))
 
         def product(acc, lhs_codes, lhs_scales, x, b):
             for n in range(N_TILES):
@@ -254,7 +261,7 @@ def tile_list_allergen_component_reading_kernel(
         last = ROW_TILES - 1
         product(yb, wb_codes[:, 0, :], wb_sc[:, 0, :], xq["b", 0], 0)
         pick_b(last)
-        xa0 = first_arm[last][:].bitcast(BF16).rearrange("p (c t) -> p c t", t=PACK)
+        xa0 = spent_whole(last)
         weave_xa(0, xa0)
         pick_a(last)
         xq["a", 0] = quantise("xa0", flat(xa0), J)

@@ -131,10 +131,10 @@ def tile_list_allergen_component_reading_kernel(
             wq[which, b, u] = quantise(f"w{which}_{b}{u}", grouped[:].rearrange("p t m i -> p (t m i)"), 2 * P)
 
         def woven(tile):
-            return tile[:].rearrange("p (c e) t -> p c t e", e=2)
+            return tile[:].rearrange("p (c e) t -> p c t e", e=4)
 
         def planes(tile):
-            return tile[:].rearrange("p t (c e) -> p c t e", e=2)
+            return tile[:].rearrange("p t (c e) -> p c t e", e=4)
 
         def flat(tile):
             return tile[:].rearrange("p c t -> p (c t)")
@@ -201,7 +201,7 @@ def tile_list_allergen_component_reading_kernel(
         def weave_xb(b):
             xb = kept(f"xb{b}", [P, J, PACK], BF16)
             for part in range(2):
-                c = slice(P * part, P * (part + 1))
+                c = slice(64 * part, 64 * (part + 1))
                 nc.scalar.copy(woven(xb)[:, c], planes(xb_planes[b])[:, c])
             return xb
 
@@ -210,7 +210,7 @@ def tile_list_allergen_component_reading_kernel(
 
         def prepare_wa(b, grouped):
             for part in range(2):
-                c = slice(P * part, P * (part + 1))
+                c = slice(64 * part, 64 * (part + 1))
                 nc.scalar.copy(woven(grouped)[:, c], planes(wa_raw[b])[:, c])
             waq[b] = quantise(f"wa{b}", flat(grouped), N)
 

from contextlib import ExitStack

import concourse.mybir as mybir

K, T, S, H, J, N = 512, 4096, 1024, 1024, 512, 512
FLOPS = 2 * (4 * K * H * S + 2 * H * N * J)

F32 = mybir.dt.float32
BF16 = mybir.dt.bfloat16
I32 = mybir.dt.int32
U32 = mybir.dt.uint32
U16 = mybir.dt.uint16
U8 = mybir.dt.uint8
FP8X4 = mybir.dt.float8_e4m3fn_x4
FP4X4 = mybir.dt.float4_e2m1fn_x4
ALU = mybir.AluOpType
ACT = mybir.ActivationFunctionType

P = 128
PACK = 4
BANK = 512
PASSES = H // (P * PACK)
ROW_TILES = H // P
HALVES = S // BANK
N_TILES = N // P


def tile_list_allergen_component_reading_kernel(
    tc, tab_words, tab_scales, offs, pos1, pos2, w1, w2, w3_words, w3_scales,
    ga, gb, food, wa, wb_words, wb_scales, out,
):
    nc = tc.nc
    with ExitStack() as ctx:
        keep = ctx.enter_context(tc.tile_pool(name="keep", bufs=1))
        staged = ctx.enter_context(tc.tile_pool(name="staged", bufs=4))
        work = ctx.enter_context(tc.tile_pool(name="work", bufs=3))
        psum = ctx.enter_context(tc.psum_pool(name="psum", bufs=1))

        def kept(name, shape, dtype):
            return keep.tile(shape, dtype, name=name, align_bytes=64)

        def stage(name, shape, dtype):
            return staged.tile(shape, dtype, name=name, tag="staged", align_bytes=64)

        def load_scale_rows(queue, plane, rows):
            nc.vector.memset(plane[:].bitcast(I32), 0)
            for q in range(4):
                queue.dma_start(plane[32 * q : 32 * q + 4].bitcast(I32), rows[4 * q : 4 * q + 4].bitcast(I32))

        def load_rows(name, matrix, b):
            raw = stage(name, [P, PACK, BANK], F32)
            nc.sync.dma_start(raw[:], matrix[BANK * b : BANK * (b + 1), :].rearrange("(p i) c -> p i c", i=PACK))
            return raw

        def load_weight_columns(name, w, b):
            raw = stage(name, [P, PACK, BANK], F32)
            nc.sync.dma_start(raw[:], w[:, BANK * b : BANK * (b + 1)].rearrange("(p i) c -> p i c", i=PACK))
            return raw

        def quantise(name, grouped, width):
            codes = kept(name + "_codes", [P, width], U32)
            scales = kept(name + "_scales", [P, width], U8)
            nc.vector.quantize_mx(out=codes[:].bitcast(FP8X4), scales=scales[:], in_=grouped)
            return codes, scales

        offs_t = kept("offs_t", [P, S // 16], U16)
        nc.sync.dma_start(offs_t[:], offs)
        w3_raw = stage("w3_raw", [P, 2 * H], U8)
        nc.sync.dma_start(w3_raw[:].bitcast(I32), w3_words[0].bitcast(I32))
        tab_w = kept("tab_w", [P, T], U32)
        tab_dram = tab_words[0].rearrange("p t i -> p (t i)").bitcast(I32)
        nc.sync.dma_start(tab_w[:, : T // 2].bitcast(I32), tab_dram[:, : T // 2])
        tab_s = kept("tab_s", [P, T], U8)
        load_scale_rows(nc.sync, tab_s, tab_scales[0])
        w_raw = {}
        w_raw[1, 0] = load_weight_columns("w1_raw0", w1, 0)
        w3s_raw = kept("w3s_raw", [P, H], U8)
        load_scale_rows(nc.sync, w3s_raw, w3_scales[0])
        nc.sync.dma_start(tab_w[:, T // 2 :].bitcast(I32), tab_dram[:, T // 2 :])
        pos2_t = kept("pos2_t", [P, J // 16], U16)
        nc.sync.dma_start(pos2_t[:], pos2)
        pos1_t = kept("pos1_t", [P, J // 16], U16)
        nc.sync.dma_start(pos1_t[:], pos1)
        w_raw[2, 0] = load_weight_columns("w2_raw0", w2, 0)
        ga_t = kept("ga_t", [P, PASSES, PACK], F32)
        nc.scalar.dma_start(ga_t[:], ga.rearrange("(b p i) -> p b i", p=P, i=PACK))
        gb_t = kept("gb_t", [P, PASSES, PACK], F32)
        nc.scalar.dma_start(gb_t[:], gb.rearrange("(b p i) -> p b i", p=P, i=PACK))

        ga_wide = kept("ga_wide", [P, ROW_TILES, J], F32)
        ga_spread = [ga_t[:, b, :].unsqueeze(2).to_broadcast([P, PACK, J]) for b in range(PASSES)]
        nc.scalar.activation(ga_wide[:, :PACK, :], ga_spread[0], ACT.Copy)
        nc.scalar.activation(ga_wide[:, PACK:, :], ga_spread[1], ACT.Copy)

        w3_codes = kept("w3_codes", [P, 2 * H], U8)
        nc.vector.tensor_copy(
            w3_codes[:].rearrange("p (b t m y) -> p b t m y", b=PASSES, t=PACK, y=2),
            w3_raw[:].rearrange("p (b m t y) -> p b t m y", b=PASSES, t=PACK, y=2),
        )

        w3_sc = kept("w3_sc", [P, H], U8)
        nc.vector.tensor_copy(
            w3_sc[:].rearrange("p (b t m) -> p b t m", b=PASSES, t=PACK),
            w3s_raw[:].rearrange("p (b m t) -> p b t m", b=PASSES, t=PACK),
        )

        w_raw[1, 1] = load_weight_columns("w1_raw1", w1, 1)
        w_raw[2, 1] = load_weight_columns("w2_raw1", w2, 1)

        v_codes, v_scales = [], []
        for half in range(HALVES):
            cols = offs_t[:, half * (BANK // 16) : (half + 1) * (BANK // 16)]
            codes = kept(f"v_codes{half}", [P, BANK], U32)
            nc.vector.tensor_copy(codes[:], tab_w[:].indirect(cols))
            scales = kept(f"v_scales{half}", [P, BANK], U8)
            nc.vector.tensor_copy(scales[:], tab_s[:].indirect(cols))
            v_codes.append(codes)
            v_scales.append(scales)

        wq = {}

        def prepare_weight(which, b, u, on_vector, grouped=None):
            if grouped is None:
                grouped = work.tile([P, 2, P, PACK], BF16, name="w_grouped", tag="w_grouped", align_bytes=64)
            src = w_raw[which, b][:].rearrange("p i (m t) -> p m i t", t=PACK)[:, :, :, 2 * u : 2 * u + 2]
            dst = grouped[:].rearrange("p t m i -> p m i t")
            if on_vector:
                nc.vector.tensor_copy(dst, src)
            else:
                nc.scalar.activation(dst, src, ACT.Copy)
            wq[which, b, u] = quantise(f"w{which}_{b}{u}", grouped[:].rearrange("p t m i -> p (t m i)"), 2 * P)

        def woven(tile):
            return tile[:].rearrange("p (c e) t -> p c t e", e=4)

        def planes(tile):
            return tile[:].rearrange("p t (c e) -> p c t e", e=4)

        def flat(tile):
            return tile[:].rearrange("p c t -> p (c t)")

        banks = [psum.tile([P, BANK], F32, name=f"bank{index}") for index in range(8)]

        def arm_bank(which, r, half):
            if r == 0:
                pair = which - 1
            elif which == 1:
                pair = 1 if r < 3 else r % 2
            else:
                pair = 2 + r % 2
            return banks[2 * pair + half]

        def arm(which, r, half):
            b, t = divmod(r, PACK)
            codes, scales = wq[which, b, t // 2]
            cols = slice(P * (t % 2), P * (t % 2 + 1))
            acc = arm_bank(which, r, half)
            nc.tensor.matmul_mx(
                out=acc[:], lhsT=codes[:, cols].bitcast(FP8X4), lhsT_scale=scales[:, cols],
                rhs=v_codes[half][:].bitcast(FP8X4), rhs_scale=v_scales[half][:], start=True, stop=False,
            )
            nc.tensor.matmul_mx(
                out=acc[:], lhsT=w3_codes[:, 2 * P * r : 2 * P * (r + 1)].bitcast(FP4X4),
                lhsT_scale=w3_sc[:, P * r : P * (r + 1)],
                rhs=v_codes[half][:].bitcast(FP8X4), rhs_scale=v_scales[half][:], start=False, stop=True,
            )
            return acc

        first_arm, h_tiles = {}, {}

        def first_arm_out(r):
            first_arm[r] = work.tile([P, S], F32, name="first_arm", tag="first_arm", align_bytes=64, bufs=5)
            for half in range(HALVES):
                acc = arm(1, r, half)
                nc.scalar.copy(first_arm[r][:, BANK * half : BANK * (half + 1)], acc[:])

        def larger_arm(r):
            h_tiles[r] = work.tile([P, S], F32, name="h", tag="h")
            for half in range(HALVES):
                cols = slice(BANK * half, BANK * (half + 1))
                acc = arm(2, r, half)
                nc.vector.tensor_tensor(h_tiles[r][:, cols], acc[:], first_arm[r][:, cols], ALU.max)

        gained_a = [kept(f"gained_a{b}", [P, PACK, J], F32) for b in range(PASSES)]
        xb_planes = [kept(f"xb_planes{b}", [P, PACK, J], BF16) for b in range(PASSES)]

        def pick_b(r):
            b, t = divmod(r, PACK)
            picked = work.tile([P, J], F32, name="picked_b", tag="picked_b")[:]
            nc.vector.tensor_copy(picked, h_tiles[r][:].indirect(pos2_t[:]))
            bent = work.tile([P, J], F32, name="bent", tag="bent")
            nc.scalar.activation(bent[:], picked, ACT.Tanh)
            nc.scalar.activation(xb_planes[b][:, t, :], bent[:], ACT.Copy, scale=gb_t[:, b, t : t + 1])

        def pick_a(r):
            b, t = divmod(r, PACK)
            nc.vector.tensor_tensor(gained_a[b][:, t, :], h_tiles[r][:].indirect(pos1_t[:]), ga_wide[:, r, :], ALU.mult)

        xq, food_raw, wa_raw, waq = {}, {}, {}, {}

        def weave_xb(b):
            xb = kept(f"xb{b}", [P, J, PACK], BF16)
            for part in range(2):
                c = slice(64 * part, 64 * (part + 1))
                nc.scalar.copy(woven(xb)[:, c], planes(xb_planes[b])[:, c])
            return xb

        def weave_xa(b, xa):
            nc.vector.tensor_tensor(woven(xa), planes(gained_a[b]), planes(food_raw[b]), ALU.add)

        def prepare_wa(b, grouped):
            for part in range(2):
                c = slice(64 * part, 64 * (part + 1))
                nc.scalar.copy(woven(grouped)[:, c], planes(wa_raw[b])[:, c])
            waq[b] = quantise(f"wa{b}", flat(grouped), N)

        def spent_half(r, half):
            spent = first_arm[r][:, BANK * half : BANK * (half + 1)]
            return spent.bitcast(BF16).rearrange("p (t m i) -> p t m i", t=2, i=PACK)

        def spent_whole(r):
            return first_arm[r][:].bitcast(BF16).rearrange("p (c t) -> p c t", t=PACK)

        prepare_weight(1, 0, 0, False)
        first_arm_out(0)
        prepare_weight(2, 0, 0, True)
        larger_arm(0)
        prepare_weight(1, 0, 1, False)
        prepare_weight(2, 0, 1, False, spent_half(0, 0))
        wa_raw[0] = load_rows("wa0", wa, 0)
        wa_raw[1] = load_rows("wa1", wa, 1)
        food_raw[0] = load_rows("food0", food, 0)
        food_raw[1] = load_rows("food1", food, 1)
        wb_codes = stage("wb_codes", [P, PASSES, N], U32)
        nc.sync.dma_start(wb_codes[:].bitcast(I32), wb_words.rearrange("a p c i -> p a (c i)").bitcast(I32))
        wb_sc = kept("wb_sc", [P, PASSES, N], U8)
        load_scale_rows(nc.sync, wb_sc, wb_scales.rearrange("a q c -> q a c"))
        for r in range(ROW_TILES - 1):
            first_arm_out(r + 1)
            larger_arm(r + 1)
            pick_b(r)
            pick_a(r)
            if r < 4:
                prepare_weight(1 + r % 2, 1, r // 2, False, spent_half(r, 1))
            if r == 4:
                xq["b", 0] = quantise("xb0", flat(weave_xb(0)), J)
            if r in (5, 6):
                prepare_wa(r - 5, spent_whole(r))

        def product(acc, lhs_codes, lhs_scales, x, b):
            for n in range(N_TILES):
                cols = slice(P * n, P * (n + 1))
                nc.tensor.matmul_mx(
                    out=acc[n][:], lhsT=lhs_codes[:, cols].bitcast(FP8X4), lhsT_scale=lhs_scales[:, cols],
                    rhs=x[0][:].bitcast(FP8X4), rhs_scale=x[1][:],
                    start=(b == 0), stop=(b == PASSES - 1),
                )

        yb = [banks[n] for n in (0, 1, 4, 5)]
        ya = [banks[n] for n in (2, 3, 6, 7)]
        last = ROW_TILES - 1
        product(yb, wb_codes[:, 0, :], wb_sc[:, 0, :], xq["b", 0], 0)
        pick_b(last)
        xa0 = spent_whole(last)
        weave_xa(0, xa0)
        pick_a(last)
        xq["a", 0] = quantise("xa0", flat(xa0), J)
        product(ya, waq[0][0], waq[0][1], xq["a", 0], 0)
        xa1 = kept("xa1", [P, J, PACK], BF16)
        weave_xa(1, xa1)
        xq["b", 1] = quantise("xb1", flat(weave_xb(1)), J)
        product(yb, wb_codes[:, 1, :], wb_sc[:, 1, :], xq["b", 1], 1)
        xq["a", 1] = quantise("xa1", flat(xa1), J)
        product(ya, waq[1][0], waq[1][1], xq["a", 1], 1)
        for n in range(N_TILES):
            yb_out = kept(f"yb_out{n}", [P, J], F32)
            nc.scalar.copy(yb_out[:], yb[n][:])
            result = kept(f"result{n}", [P, J], F32)
            nc.vector.scalar_tensor_tensor(result[:], ya[n][:], 1.0, yb_out[:], ALU.add, ALU.mult)
            nc.sync.dma_start(out[P * n : P * (n + 1), :], result[:])
